import numpy as np
import ml_dtypes


def mxq(x, axis, fmt="e4m3"):
    dtype, down = {"e4m3": (ml_dtypes.float8_e4m3fn, 7), "e5m2": (ml_dtypes.float8_e5m2, 14)}[fmt]
    v = np.moveaxis(np.asarray(x, np.float32).astype(ml_dtypes.bfloat16).astype(np.float64), axis, -1)
    blocks = v.reshape(v.shape[:-1] + (-1, 32))
    amax = np.abs(blocks).max(-1, keepdims=True)
    byte = np.maximum(np.where(amax > 0, np.frexp(amax)[1] - 1 + 127, 0) - down, 1)
    scale = np.exp2(byte - 127.0)
    codes = (blocks / scale).astype(np.float32).astype(dtype).astype(np.float64)
    return np.moveaxis((codes * scale).reshape(v.shape), -1, axis)


WIDE = False


def mx_kscale(k):
    if not WIDE:
        return np.ones(k)
    levels = np.array([10, -10, 5, -5, 0])
    if k % 512:
        return np.exp2(np.random.permutation(np.resize(levels, k // 32))).repeat(32)
    a = np.empty((k // 512, 16))
    for p in range(k // 512):
        a[p, :8] = np.random.permutation(np.resize(levels, 8))
        for g in range(8):
            far = levels[np.abs(levels - a[p, g]) >= 10]
            a[p, g + 8] = far[np.random.randint(len(far))]
    return np.exp2(a.ravel()).repeat(32)


BF16 = ml_dtypes.bfloat16


def bf(x):
    return np.asarray(x, np.float32).astype(BF16)


def f64(x):
    return np.asarray(x).astype(np.float64)


E2M1 = np.array([0.0, 0.5, 1.0, 1.5, 2.0, 3.0, 4.0, 6.0, -0.0, -0.5, -1.0, -1.5, -2.0, -3.0, -4.0, -6.0])


def pack_weight(w, fmt):
    k, n = w.shape
    w = f64(bf(w)).reshape(k // 32, 32, n)
    amax = np.abs(w).max(1)
    if fmt == "e4m3":
        byte = np.frexp(amax)[1] - 1 + 127 - 7
    else:
        mant, ex = np.frexp(amax / 6.0)
        byte = np.where(mant > 0.5, ex, ex - 1) + 127
    byte = np.clip(np.where(amax > 0, byte, 1), 1, 254)
    scaled = (w * np.exp2(127.0 - byte)[:, None, :]).reshape(k, n).astype(np.float32)
    by_word = np.ascontiguousarray(scaled.reshape(k // 512, 128, 4, n).transpose(0, 1, 3, 2))
    if fmt == "e4m3":
        words = by_word.astype(ml_dtypes.float8_e4m3fn).view(np.uint8)
    else:
        c = by_word.astype(ml_dtypes.float4_e2m1fn).view(np.uint8) & 0xF
        words = c[..., 0::2] | (c[..., 1::2] << 4)
    return np.ascontiguousarray(words), np.ascontiguousarray(byte.astype(np.uint8).reshape(k // 512, 16, n))


def unpack_weight(words, scales, fmt):
    g, p, n, _ = words.shape
    if fmt == "e4m3":
        vals = np.ascontiguousarray(words).view(ml_dtypes.float8_e4m3fn).astype(np.float64)
    else:
        nib = np.empty((g, p, n, 4), np.uint8)
        nib[..., 0::2] = words & 0xF
        nib[..., 1::2] = words >> 4
        vals = E2M1[nib]
    vals = vals * np.repeat(np.exp2(scales.astype(np.float64) - 127.0), 8, axis=1)[..., None]
    return vals.transpose(0, 1, 3, 2).reshape(g * 512, n)
def pack4(w):
    words, scales = pack_weight(w, "e2m1")
    return words.reshape(words.shape[0], 128, -1), scales


def unpack4(words, scales):
    return unpack_weight(words.reshape(words.shape[0], 128, -1, 2), scales, "e2m1")


def planes(Y):
    n, m = Y.shape
    b = f64(bf(Y)).reshape(n // 32, 32, m)
    amax = np.abs(b).max(1)
    byte = np.clip(np.where(amax > 0, np.frexp(amax)[1] - 1 + 127 - 7, 1), 1, 254)
    codes = (b * np.exp2(127.0 - byte)[:, None, :]).reshape(n, m).astype(np.float32).astype(ml_dtypes.float8_e4m3fn).view(np.uint8)
    words = codes.reshape(n // 512, 128, 4, m).transpose(0, 1, 3, 2)
    return np.ascontiguousarray(words), np.ascontiguousarray(byte.astype(np.uint8).reshape(n // 512, 16, m))


T, R, K, N = 8, 128, 2048, 1536


def deviations(e, axis):
    return e - e.mean(axis=axis, keepdims=True)


def setup_inputs():
    s = mx_kscale(K)
    anomalies = deviations(np.random.randn(T, R, K), 1)
    h = np.random.randn(K, N) / np.sqrt(K)
    h_words, h_scales = pack4(h / s[:, None])
    bias_anomalies = deviations(0.5 * np.random.randn(R, N), 0)
    obs_std = np.exp(np.random.uniform(-1.6, 1.6, (T, N)))
    return {
        "anomalies": bf(anomalies * s),
        "h_words": h_words,
        "h_scales": h_scales,
        "bias_anomalies": bf(bias_anomalies),
        "obs_std": bf(obs_std),
    }


def reference(anomalies, h_words, h_scales, bias_anomalies, obs_std):
    a = mxq(f64(anomalies).reshape(T * R, K), 1, "e4m3")
    h = unpack4(h_words, h_scales)
    p = (a @ h).reshape(T, R, N)
    y = (p + f64(bias_anomalies)[None, :, :]) / f64(obs_std)[:, None, :]
    Y = y.reshape(T * R, N).T
    words, scales = planes(Y)
    return y, words, scales

@@ -1,0 +1,327 @@
+from contextlib import ExitStack
+
+import concourse.mybir as mybir
+from concourse.masks import make_identity
+
+T, R, K, N = 8, 128, 2048, 1536
+FLOPS = 2 * T * R * K * N
+
+F32 = mybir.dt.float32
+BF16 = mybir.dt.bfloat16
+I32 = mybir.dt.int32
+U32 = mybir.dt.uint32
+U8 = mybir.dt.uint8
+FP8X4 = mybir.dt.float8_e4m3fn_x4
+FP4X4 = mybir.dt.float4_e2m1fn_x4
+ACT = mybir.ActivationFunctionType
+ALU = mybir.AluOpType
+
+P = 128
+PASSES = K // 512
+CHUNK = 512
+CHUNKS = N // CHUNK
+SLOTS = 4
+MEMBERS = P // SLOTS
+GROUPS = T // SLOTS
+TILES_PER_GROUP = R // MEMBERS
+TILES = GROUPS * TILES_PER_GROUP
+UNITS = TILES * CHUNKS
+STD_ROW = 8
+
+
+def tile_ensemble_observation_anomalies_g4_kernel(
+    tc, anomalies, h_words, h_scales, bias_anomalies, obs_std, out_0, out_1, out_2
+):
+    nc = tc.nc
+
+    def rows_of(tensor, i):
+        g, j = divmod(i, TILES_PER_GROUP)
+        return tensor[SLOTS * g : SLOTS * (g + 1), MEMBERS * j : MEMBERS * (j + 1), :].rearrange("d e x -> e d x")
+
+    with ExitStack() as ctx:
+        keep = ctx.enter_context(tc.tile_pool(name="keep", bufs=1))
+        work = ctx.enter_context(tc.tile_pool(name="work", bufs=1))
+        psum = ctx.enter_context(tc.psum_pool(name="psum", bufs=1))
+        ctx.enter_context(tc.manual_schedule())
+
+        ident = keep.tile([P, P], F32, name="ident")
+        select = keep.tile([P, P], BF16, name="select")
+        one = keep.tile([P, 1], F32, name="one")
+        one_out = keep.tile([P, 1], F32, name="one_out")
+        std_rows = keep.tile([P, N], BF16, name="std_rows")
+        std_late = keep.tile([P, N], BF16, name="std_late")
+        h_codes = [keep.tile([P, 2 * N], U8, name="h_codes%d" % g, align_bytes=64) for g in range(PASSES)]
+        h_planes = [keep.tile([P, 2, N], U8, name="h_planes%d" % h, align_bytes=64) for h in range(2)]
+        bias = [keep.tile([P, N], BF16, name="bias%d" % j) for j in range(TILES_PER_GROUP)]
+        recip = [[keep.tile([P, CHUNK], F32, name="recip%d_%d" % (g, c)) for c in range(CHUNKS)] for g in range(GROUPS)]
+        first_halves = [keep.tile([P, K // 2], BF16, name="first%d" % h) for h in range(2)]
+        raw = [None] + [keep.tile([P, K], BF16, name="raw%d" % i) for i in range(1, TILES)]
+        y_turned = [
+            [keep.tile([P, 4 * CHUNK], BF16, name="y_turned%d_%d" % (g, c), align_bytes=64) for c in range(CHUNKS)]
+            for g in range(GROUPS)
+        ]
+        y_codes = [
+            [keep.tile([P, CHUNK], U32, name="y_codes%d_%d" % (g, c), align_bytes=64) for c in range(CHUNKS)]
+            for g in range(GROUPS)
+        ]
+        y_planes = [keep.tile([P, CHUNKS, CHUNK], U8, name="y_planes%d" % g, align_bytes=64) for g in range(GROUPS)]
+
+        a_banks, grouped, a_codes, a_planes = {}, {}, {}, {}
+        acc, summed, y_rows, y_sorted, y_banks, roots = {}, {}, {}, {}, {}, {}
+
+        def load_a(i):
+            nc.sync.dma_start(out=raw[i][:], in_=rows_of(anomalies, i))
+
+        def load_first(h):
+            nc.sync.dma_start(out=first_halves[h][:], in_=rows_of(anomalies, 0)[:, :, h * (K // 2) : (h + 1) * (K // 2)])
+
+        def load_h(g):
+            nc.sync.dma_start(out=h_codes[g][:].bitcast(I32), in_=h_words[g].bitcast(I32))
+
+        def load_h_scales(h):
+            for q in range(4):
+                nc.sync.dma_start(
+                    out=h_planes[h][32 * q : 32 * q + 4, :, :].bitcast(I32),
+                    in_=h_scales[2 * h : 2 * h + 2, 4 * q : 4 * q + 4, :].rearrange("g r n -> r g n").bitcast(I32),
+                )
+
+        def load_bias(j):
+            src = bias_anomalies[MEMBERS * j : MEMBERS * (j + 1), :].unsqueeze(1).broadcast_to([MEMBERS, SLOTS, N])
+            nc.sync.dma_start(out=bias[j][:], in_=src)
+
+        def transpose_a(i, h):
+            src = first_halves[h][:] if i == 0 else raw[i][:, h * (K // 2) : (h + 1) * (K // 2)]
+            words = src.bitcast(F32)
+            bank = psum.tile([P, 2, 2, P], F32, name="a_bank", tag="a_bank%d" % h)
+            a_banks[i, h] = bank
+            for g in range(2):
+                for u in range(2):
+                    nc.tensor.transpose(bank[:, g, u, :], words[:, 256 * g + u : 256 * (g + 1) : 2], ident[:])
+
+        def evacuate_a(i, h):
+            if h == 0:
+                grouped[i] = work.tile([P, K], BF16, name="grouped", tag="grouped", bufs=2, align_bytes=64)
+            dst = grouped[i][:, h * (K // 2) : (h + 1) * (K // 2)].bitcast(F32)
+            nc.scalar.copy(
+                out=dst.rearrange("p (g r u) -> p g r u", g=2, u=2),
+                in_=a_banks[i, h][:].rearrange("p g u r -> p g r u"),
+            )
+
+        def quantize_a(i, lo, hi):
+            if lo == 0:
+                a_codes[i] = work.tile([P, PASSES * P], U32, name="a_codes", tag="a_codes", bufs=3, align_bytes=64)
+                a_planes[i] = work.tile([P, PASSES * P], U8, name="a_planes", tag="a_planes", bufs=3, align_bytes=64)
+            nc.vector.quantize_mx(
+                out=a_codes[i][:, lo * P : hi * P].bitcast(FP8X4),
+                scales=a_planes[i][:, lo * P : hi * P],
+                in_=grouped[i][:, lo * 4 * P : hi * 4 * P],
+            )
+
+        def mx_pass(i, c, g):
+            u = CHUNKS * i + c
+            if g == 0:
+                acc[u] = psum.tile([P, CHUNK], F32, name="acc", tag="acc", bufs=4)
+            nc.tensor.matmul_mx(
+                out=acc[u][:],
+                lhsT=a_codes[i][:, g * P : (g + 1) * P].bitcast(FP8X4),
+                lhsT_scale=a_planes[i][:, g * P : (g + 1) * P],
+                rhs=h_codes[g][:, 2 * CHUNK * c : 2 * CHUNK * (c + 1)].bitcast(FP4X4),
+                rhs_scale=h_planes[g // 2][:, g % 2, CHUNK * c : CHUNK * (c + 1)],
+                start=(g == 0),
+                stop=(g == PASSES - 1),
+            )
+
+        def multiply(u):
+            i, c = divmod(u, CHUNKS)
+            for g in range(PASSES):
+                mx_pass(i, c, g)
+
+        def add_bias(u):
+            i, c = divmod(u, CHUNKS)
+            summed[u] = work.tile([P, CHUNK], F32, name="summed", tag="summed", bufs=4)
+            nc.vector.tensor_tensor(
+                out=summed[u][:], in0=acc[u][:], in1=bias[i % TILES_PER_GROUP][:, CHUNK * c : CHUNK * (c + 1)], op=ALU.add
+            )
+
+        def scale(u):
+            i, c = divmod(u, CHUNKS)
+            if c == 0:
+                y_rows[i] = work.tile([P, N], F32, name="y_rows", tag="y_rows", bufs=5)
+            nc.vector.tensor_tensor(
+                out=y_rows[i][:, CHUNK * c : CHUNK * (c + 1)],
+                in0=summed[u][:],
+                in1=recip[i // TILES_PER_GROUP][c][:],
+                op=ALU.mult,
+            )
+
+        def store_y(i, lo, hi):
+            nc.sync.dma_start(
+                out=rows_of(out_0, i)[:, :, CHUNK * lo : CHUNK * hi], in_=y_rows[i][:, CHUNK * lo : CHUNK * hi]
+            )
+
+        def round_y(u):
+            i, c = divmod(u, CHUNKS)
+            y_sorted[u] = work.tile([P, CHUNK], BF16, name="y_sorted", tag="y_sorted", bufs=8)
+            nc.scalar.copy(
+                out=y_sorted[u][:].rearrange("t (u p e) -> t u p e", u=2, e=2),
+                in_=y_rows[i][:, CHUNK * c : CHUNK * (c + 1)].rearrange("t (p u e) -> t u p e", u=2, e=2),
+            )
+
+        def transpose_y(units):
+            for n, u in enumerate(units):
+                if n % 2 == 0:
+                    bank = psum.tile([P, 2, 2, P], F32, name="y_bank", tag="y_bank%d" % (n // 2), bufs=1)
+                y_banks[u] = bank[:, n % 2, :, :]
+                words = y_sorted[u][:].bitcast(F32)
+                for h in range(2):
+                    nc.tensor.transpose(bank[:, n % 2, h, :], words[:, h * P : (h + 1) * P], ident[:])
+
+        def evacuate_y(u):
+            i, c = divmod(u, CHUNKS)
+            g, j = divmod(i, TILES_PER_GROUP)
+            dst = y_turned[g][c][:].bitcast(F32).rearrange("p (d m u) -> p d m u", d=SLOTS, u=2)
+            nc.scalar.copy(
+                out=dst[:, :, MEMBERS * j : MEMBERS * (j + 1), :],
+                in_=y_banks[u].rearrange("p u (e d) -> p d e u", d=SLOTS),
+            )
+
+        def quantize_y(g, c):
+            nc.vector.quantize_mx(out=y_codes[g][c][:].bitcast(FP8X4), scales=y_planes[g][:, c, :], in_=y_turned[g][c][:])
+
+        def store_codes(g, c):
+            dst = out_1[c].rearrange("p m t -> p (m t)")[:, 4 * CHUNK * g : 4 * CHUNK * (g + 1)]
+            nc.sync.dma_start(out=dst.bitcast(I32), in_=y_codes[g][c][:].bitcast(I32))
+
+        def store_scales(g, engines):
+            for q in range(4):
+                dst = out_2[:, 4 * q : 4 * q + 4, CHUNK * g : CHUNK * (g + 1)].rearrange("c r m -> r c m")
+                engines[q].dma_start(out=dst.bitcast(I32), in_=y_planes[g][32 * q : 32 * q + 4, :, :].bitcast(I32))
+
+        def root(g, c, src):
+            roots[g, c] = work.tile([P, CHUNK], F32, name="roots", tag="roots", bufs=3)
+            nc.scalar.activation(out=roots[g, c][:], in_=src, func=ACT.Abs_reciprocal_sqrt)
+
+        def square(g, c):
+            nc.scalar.activation(out=recip[g][c][:], in_=roots[g, c][:], func=ACT.Square)
+
+        nc.vector.memset(one[:], 1.0)
+        nc.vector.memset(h_planes[0][:].rearrange("p g n -> p (g n)").bitcast(I32), 0)
+        nc.vector.memset(std_rows[:].bitcast(I32), 0)
+        make_identity(nc, ident[:])
+        nc.gpsimd.memset(h_planes[1][:].rearrange("p g n -> p (g n)").bitcast(I32), 0)
+        nc.scalar.activation(out=one_out[:], in_=one[:], func=ACT.Abs_reciprocal_sqrt)
+        nc.vector.tensor_copy(
+            out=select[:].rearrange("k (e d) -> k e d", d=SLOTS),
+            in_=ident[:, STD_ROW : STD_ROW + SLOTS].unsqueeze(1).broadcast_to([P, MEMBERS, SLOTS]),
+        )
+
+        load_first(0)
+        load_h(0)
+        load_h_scales(0)
+        nc.sync.dma_start(out=std_rows[STD_ROW : STD_ROW + SLOTS, :], in_=obs_std[0:SLOTS, :])
+        load_first(1)
+        load_h(1)
+        load_a(1)
+        load_h_scales(1)
+        load_h(2)
+        load_h(3)
+        load_bias(0)
+        load_a(2)
+        load_bias(1)
+        load_a(3)
+        nc.sync.dma_start(out=std_late[:], in_=obs_std[SLOTS : 2 * SLOTS, :].unsqueeze(0).broadcast_to([MEMBERS, SLOTS, N]))
+        load_bias(2)
+        load_a(4)
+        load_bias(3)
+        for i in range(5, TILES):
+            load_a(i)
+
+        for h in range(2):
+            transpose_a(0, h)
+            evacuate_a(0, h)
+            quantize_a(0, 2 * h, 2 * h + 2)
+        for c in range(CHUNKS):
+            tag = "acc" if c == 0 else "y_bank%d" % (c - 1)
+            spread = psum.tile([P, CHUNK], F32, name="spread", tag=tag, bufs=4 if c == 0 else 1)
+            nc.tensor.matmul(spread[:], lhsT=select[:], rhs=std_rows[:, CHUNK * c : CHUNK * (c + 1)], start=True, stop=True)
+            root(0, c, spread[:])
+        for g in range(PASSES):
+            if g == 2:
+                for h in range(2):
+                    transpose_a(1, h)
+                    evacuate_a(1, h)
+                quantize_a(1, 0, PASSES)
+            for c in range(CHUNKS):
+                mx_pass(0, c, g)
+        for c in range(CHUNKS):
+            square(0, c)
+        add_bias(0)
+        add_bias(1)
+        scale(0)
+        round_y(0)
+
+        for i in range(1, TILES):
+            u = CHUNKS * i
+            last = i == TILES - 1
+            if i == 1:
+                multiply(u)
+            if not last:
+                for h in range(2):
+                    transpose_a(i + 1, h)
+                    evacuate_a(i + 1, h)
+            add_bias(u - 1)
+            scale(u - 2)
+            turned = list(range(max(u - 5, 0) if i > 2 else 0, u - 2)) if i > 1 else []
+            transpose_y(turned)
+            round_y(u - 2)
+            scale(u - 1)
+            store_y(i - 1, 0, CHUNKS)
+            round_y(u - 1)
+            for v in turned:
+                evacuate_y(v)
+            if i <= CHUNKS:
+                root(1, i - 1, std_late[:, CHUNK * (i - 1) : CHUNK * i])
+                square(1, i - 1)
+            if i >= 5:
+                quantize_y(0, i - 5)
+                store_codes(0, i - 5)
+            if i != 1:
+                multiply(u)
+            add_bias(u)
+            if not last:
+                quantize_a(i + 1, 0, PASSES)
+            else:
+                store_scales(0, [nc.sync] * 4)
+            multiply(u + 1)
+            scale(u)
+            round_y(u)
+            add_bias(u + 1)
+            multiply(u + 2)
+
+        i = TILES - 1
+        u = UNITS
+        store_y(i, 0, 1)
+        add_bias(u - 1)
+        scale(u - 2)
+        transpose_y([u - 5, u - 4, u - 3])
+        for v in range(u - 5, u - 2):
+            evacuate_y(v)
+        store_y(i, 1, 2)
+        scale(u - 1)
+        store_y(i, 2, 3)
+        round_y(u - 2)
+        round_y(u - 1)
+        quantize_y(1, 0)
+        store_codes(1, 0)
+        transpose_y([u - 2])
+        evacuate_y(u - 2)
+        quantize_y(1, 1)
+        store_codes(1, 1)
+        bank_last = psum.tile([P, 2, P], F32, name="bank_last", tag="y_bank1", bufs=1)
+        y_banks[u - 1] = bank_last[:]
+        for h in range(2):
+            nc.tensor.transpose(bank_last[:, h, :], y_sorted[u - 1][:].bitcast(F32)[:, h * P : (h + 1) * P], ident[:])
+        evacuate_y(u - 1)
+        quantize_y(1, 2)
+        store_codes(1, 2)
+        store_scales(1, [nc.scalar, nc.scalar, nc.sync, nc.sync])

@@ -26,7 +26,21 @@ GROUPS = T // SLOTS
 TILES_PER_GROUP = R // MEMBERS
 TILES = GROUPS * TILES_PER_GROUP
 UNITS = TILES * CHUNKS
+PAIRS = UNITS // 2
 STD_ROW = 8
+WARM_UPS = 4
+LAG = 2
+RUNS = [1, 3, 4, 5, 6, 9, 11]
+
+
+ORDER = [(0, 0, 0), (0, 1, 0), (0, 0, 2), (0, 1, 2), (0, 2, 0), (0, 2, 2)] + [
+    (1, c, j) for c in range(CHUNKS) for j in (0, 2)
+]
+
+
+def place(n):
+    g, c, j = ORDER[n // 2]
+    return g, c, j + n % 2
 
 
 def tile_ensemble_observation_anomalies_g4_kernel(
@@ -34,8 +48,7 @@ def tile_ensemble_observation_anomalies_g4_kernel(
 ):
     nc = tc.nc
 
-    def rows_of(tensor, i):
-        g, j = divmod(i, TILES_PER_GROUP)
+    def rows_of(tensor, g, j):
         return tensor[SLOTS * g : SLOTS * (g + 1), MEMBERS * j : MEMBERS * (j + 1), :].rearrange("d e x -> e d x")
 
     with ExitStack() as ctx:
@@ -45,283 +58,290 @@ def tile_ensemble_observation_anomalies_g4_kernel(
         ctx.enter_context(tc.manual_schedule())
 
         ident = keep.tile([P, P], F32, name="ident")
-        select = keep.tile([P, P], BF16, name="select")
+        by_slot = keep.tile([P, P], F32, name="by_slot")
+        select = [keep.tile([P, P], BF16, name="select%d" % g) for g in range(GROUPS)]
         one = keep.tile([P, 1], F32, name="one")
         one_out = keep.tile([P, 1], F32, name="one_out")
         std_rows = keep.tile([P, N], BF16, name="std_rows")
-        std_late = keep.tile([P, N], BF16, name="std_late")
-        h_codes = [keep.tile([P, 2 * N], U8, name="h_codes%d" % g, align_bytes=64) for g in range(PASSES)]
-        h_planes = [keep.tile([P, 2, N], U8, name="h_planes%d" % h, align_bytes=64) for h in range(2)]
-        bias = [keep.tile([P, N], BF16, name="bias%d" % j) for j in range(TILES_PER_GROUP)]
-        recip = [[keep.tile([P, CHUNK], F32, name="recip%d_%d" % (g, c)) for c in range(CHUNKS)] for g in range(GROUPS)]
+        h_codes = [keep.tile([P, PASSES, 2 * CHUNK], U8, name="h_codes%d" % c, align_bytes=256) for c in range(CHUNKS)]
+        h_planes = [keep.tile([P, PASSES, CHUNK], U8, name="h_planes%d" % c, align_bytes=256) for c in range(CHUNKS)]
+        bias = [[keep.tile([P, CHUNK], BF16, name="bias%d_%d" % (j, c)) for c in range(CHUNKS)] for j in range(TILES_PER_GROUP)]
         first_halves = [keep.tile([P, K // 2], BF16, name="first%d" % h) for h in range(2)]
         raw = [None] + [keep.tile([P, K], BF16, name="raw%d" % i) for i in range(1, TILES)]
-        y_turned = [
-            [keep.tile([P, 4 * CHUNK], BF16, name="y_turned%d_%d" % (g, c), align_bytes=64) for c in range(CHUNKS)]
-            for g in range(GROUPS)
-        ]
+        a_codes = [keep.tile([P, PASSES * P], U32, name="a_codes%d" % i, align_bytes=256) for i in range(TILES)]
+        a_planes = [keep.tile([P, PASSES * P], U8, name="a_planes%d" % i, align_bytes=256) for i in range(TILES)]
         y_codes = [
             [keep.tile([P, CHUNK], U32, name="y_codes%d_%d" % (g, c), align_bytes=64) for c in range(CHUNKS)]
             for g in range(GROUPS)
         ]
         y_planes = [keep.tile([P, CHUNKS, CHUNK], U8, name="y_planes%d" % g, align_bytes=64) for g in range(GROUPS)]
 
-        a_banks, grouped, a_codes, a_planes = {}, {}, {}, {}
-        acc, summed, y_rows, y_sorted, y_banks, roots = {}, {}, {}, {}, {}, {}
+        a_banks, grouped, spreads, recip = {}, {}, {}, {}
+        acc, summed, y_rows, y_sorted, y_banks, y_turned = {}, {}, {}, {}, {}, {}
 
         def load_a(i):
-            nc.sync.dma_start(out=raw[i][:], in_=rows_of(anomalies, i))
+            nc.sync.dma_start(out=raw[i][:], in_=rows_of(anomalies, *divmod(i, TILES_PER_GROUP)))
 
         def load_first(h):
-            nc.sync.dma_start(out=first_halves[h][:], in_=rows_of(anomalies, 0)[:, :, h * (K // 2) : (h + 1) * (K // 2)])
+            nc.sync.dma_start(out=first_halves[h][:], in_=rows_of(anomalies, 0, 0)[:, :, h * (K // 2) : (h + 1) * (K // 2)])
 
-        def load_h(g):
-            nc.sync.dma_start(out=h_codes[g][:].bitcast(I32), in_=h_words[g].bitcast(I32))
+        def load_h(c):
+            src = h_words[:, :, 2 * CHUNK * c : 2 * CHUNK * (c + 1)].rearrange("g p x -> p g x")
+            nc.sync.dma_start(out=h_codes[c][:].bitcast(I32), in_=src.bitcast(I32))
 
-        def load_h_scales(h):
-            for q in range(4):
-                nc.sync.dma_start(
-                    out=h_planes[h][32 * q : 32 * q + 4, :, :].bitcast(I32),
-                    in_=h_scales[2 * h : 2 * h + 2, 4 * q : 4 * q + 4, :].rearrange("g r n -> r g n").bitcast(I32),
-                )
+        def load_h_scales(c):
+            for r in range(4):
+                src = h_scales[:, r:16:4, CHUNK * c : CHUNK * (c + 1)].rearrange("g q n -> q g n")
+                nc.sync.dma_start(out=h_planes[c][r:P:32, :, :].bitcast(I32), in_=src.bitcast(I32))
 
-        def load_bias(j):
-            src = bias_anomalies[MEMBERS * j : MEMBERS * (j + 1), :].unsqueeze(1).broadcast_to([MEMBERS, SLOTS, N])
-            nc.sync.dma_start(out=bias[j][:], in_=src)
+        def load_bias(c, first):
+            for j in (first, first + 1):
+                src = bias_anomalies[MEMBERS * j : MEMBERS * (j + 1), CHUNK * c : CHUNK * (c + 1)]
+                nc.sync.dma_start(out=bias[j][c][:], in_=src.unsqueeze(1).broadcast_to([MEMBERS, SLOTS, CHUNK]))
 
         def transpose_a(i, h):
             src = first_halves[h][:] if i == 0 else raw[i][:, h * (K // 2) : (h + 1) * (K // 2)]
             words = src.bitcast(F32)
-            bank = psum.tile([P, 2, 2, P], F32, name="a_bank", tag="a_bank%d" % h)
+            bank = psum.tile([P, 2, 2, P], F32, name="a_bank", tag="turn", bufs=4)
             a_banks[i, h] = bank
             for g in range(2):
                 for u in range(2):
                     nc.tensor.transpose(bank[:, g, u, :], words[:, 256 * g + u : 256 * (g + 1) : 2], ident[:])
 
-        def evacuate_a(i, h):
+        def evacuate_a(i, h, copy):
             if h == 0:
-                grouped[i] = work.tile([P, K], BF16, name="grouped", tag="grouped", bufs=2, align_bytes=64)
+                grouped[i] = work.tile([P, K], BF16, name="grouped", tag="grouped", bufs=3, align_bytes=64)
             dst = grouped[i][:, h * (K // 2) : (h + 1) * (K // 2)].bitcast(F32)
-            nc.scalar.copy(
+            copy(
                 out=dst.rearrange("p (g r u) -> p g r u", g=2, u=2),
                 in_=a_banks[i, h][:].rearrange("p g u r -> p g r u"),
             )
 
+        def turn_a(i):
+            for h in range(2):
+                transpose_a(i, h)
+                evacuate_a(i, h, nc.scalar.copy)
+
         def quantize_a(i, lo, hi):
-            if lo == 0:
-                a_codes[i] = work.tile([P, PASSES * P], U32, name="a_codes", tag="a_codes", bufs=3, align_bytes=64)
-                a_planes[i] = work.tile([P, PASSES * P], U8, name="a_planes", tag="a_planes", bufs=3, align_bytes=64)
             nc.vector.quantize_mx(
                 out=a_codes[i][:, lo * P : hi * P].bitcast(FP8X4),
                 scales=a_planes[i][:, lo * P : hi * P],
                 in_=grouped[i][:, lo * 4 * P : hi * 4 * P],
             )
 
-        def mx_pass(i, c, g):
-            u = CHUNKS * i + c
-            if g == 0:
-                acc[u] = psum.tile([P, CHUNK], F32, name="acc", tag="acc", bufs=4)
-            nc.tensor.matmul_mx(
-                out=acc[u][:],
-                lhsT=a_codes[i][:, g * P : (g + 1) * P].bitcast(FP8X4),
-                lhsT_scale=a_planes[i][:, g * P : (g + 1) * P],
-                rhs=h_codes[g][:, 2 * CHUNK * c : 2 * CHUNK * (c + 1)].bitcast(FP4X4),
-                rhs_scale=h_planes[g // 2][:, g % 2, CHUNK * c : CHUNK * (c + 1)],
-                start=(g == 0),
-                stop=(g == PASSES - 1),
-            )
+        def multiply(n):
+            g, c, j = place(n)
+            i = TILES_PER_GROUP * g + j
+            acc[n] = psum.tile([P, CHUNK], F32, name="acc", tag="acc", bufs=4)
+            for s in range(PASSES):
+                nc.tensor.matmul_mx(
+                    out=acc[n][:],
+                    lhsT=a_codes[i][:, s * P : (s + 1) * P].bitcast(FP8X4),
+                    lhsT_scale=a_planes[i][:, s * P : (s + 1) * P],
+                    rhs=h_codes[c][:, s, :].bitcast(FP4X4),
+                    rhs_scale=h_planes[c][:, s, :],
+                    start=(s == 0),
+                    stop=(s == PASSES - 1),
+                )
 
-        def multiply(u):
-            i, c = divmod(u, CHUNKS)
-            for g in range(PASSES):
-                mx_pass(i, c, g)
+        def add_bias(n):
+            g, c, j = place(n)
+            if n % 2 == 0:
+                summed[n // 2] = work.tile([P, 2, CHUNK], F32, name="summed", tag="summed", bufs=3)
+            nc.vector.tensor_tensor(out=summed[n // 2][:, n % 2, :], in0=acc[n][:], in1=bias[j][c][:], op=ALU.add)
 
-        def add_bias(u):
-            i, c = divmod(u, CHUNKS)
-            summed[u] = work.tile([P, CHUNK], F32, name="summed", tag="summed", bufs=4)
+        def scale(k, lo, hi):
+            g, c, j = place(2 * k)
+            if lo == 0:
+                y_rows[k] = work.tile([P, 2, CHUNK], F32, name="y_rows", tag="y_rows", bufs=6)
             nc.vector.tensor_tensor(
-                out=summed[u][:], in0=acc[u][:], in1=bias[i % TILES_PER_GROUP][:, CHUNK * c : CHUNK * (c + 1)], op=ALU.add
-            )
-
-        def scale(u):
-            i, c = divmod(u, CHUNKS)
-            if c == 0:
-                y_rows[i] = work.tile([P, N], F32, name="y_rows", tag="y_rows", bufs=5)
-            nc.vector.tensor_tensor(
-                out=y_rows[i][:, CHUNK * c : CHUNK * (c + 1)],
-                in0=summed[u][:],
-                in1=recip[i // TILES_PER_GROUP][c][:],
+                out=y_rows[k][:, lo:hi, :],
+                in0=summed[k][:, lo:hi, :],
+                in1=recip[g, c][:].unsqueeze(1).broadcast_to([P, hi - lo, CHUNK]),
                 op=ALU.mult,
             )
+            for a in range(lo, hi):
+                nc.sync.dma_start(out=rows_of(out_0, g, j + a)[:, :, CHUNK * c : CHUNK * (c + 1)], in_=y_rows[k][:, a, :])
 
-        def store_y(i, lo, hi):
-            nc.sync.dma_start(
-                out=rows_of(out_0, i)[:, :, CHUNK * lo : CHUNK * hi], in_=y_rows[i][:, CHUNK * lo : CHUNK * hi]
+        def round_y(k, lo, hi):
+            if lo == 0:
+                y_sorted[k] = work.tile([P, 2 * CHUNK], BF16, name="y_sorted", tag="y_sorted", bufs=4)
+            nc.scalar.copy(
+                out=y_sorted[k][:, CHUNK * lo : CHUNK * hi].rearrange("t (a u p e) -> t a u p e", u=2, p=P, e=2),
+                in_=y_rows[k][:, lo:hi, :].rearrange("t a (p u e) -> t a u p e", u=2, e=2),
             )
 
-        def round_y(u):
-            i, c = divmod(u, CHUNKS)
-            y_sorted[u] = work.tile([P, CHUNK], BF16, name="y_sorted", tag="y_sorted", bufs=8)
-            nc.scalar.copy(
-                out=y_sorted[u][:].rearrange("t (u p e) -> t u p e", u=2, e=2),
-                in_=y_rows[i][:, CHUNK * c : CHUNK * (c + 1)].rearrange("t (p u e) -> t u p e", u=2, e=2),
-            )
+        def transpose_y(k, lo, hi):
+            bank = psum.tile([P, 2, 2, P], F32, name="y_bank", tag="turn", bufs=4)
+            y_banks[k] = bank
+            words = y_sorted[k][:].bitcast(F32)
+            for a in range(lo, hi):
+                for u in range(2):
+                    nc.tensor.transpose(bank[:, a, u, :], words[:, (2 * a + u) * P : (2 * a + u + 1) * P], by_slot[:])
 
-        def transpose_y(units):
-            for n, u in enumerate(units):
-                if n % 2 == 0:
-                    bank = psum.tile([P, 2, 2, P], F32, name="y_bank", tag="y_bank%d" % (n // 2), bufs=1)
-                y_banks[u] = bank[:, n % 2, :, :]
-                words = y_sorted[u][:].bitcast(F32)
-                for h in range(2):
-                    nc.tensor.transpose(bank[:, n % 2, h, :], words[:, h * P : (h + 1) * P], ident[:])
-
-        def evacuate_y(u):
-            i, c = divmod(u, CHUNKS)
-            g, j = divmod(i, TILES_PER_GROUP)
-            dst = y_turned[g][c][:].bitcast(F32).rearrange("p (d m u) -> p d m u", d=SLOTS, u=2)
+        def evacuate_y(k, lo, hi):
+            g, c, j = place(2 * k)
+            if (g, c) not in y_turned:
+                y_turned[g, c] = work.tile([P, 4 * CHUNK], BF16, name="y_turned", tag="y_turned", bufs=3, align_bytes=64)
+            dst = y_turned[g, c][:].bitcast(F32).rearrange("p (d a e u) -> p a d e u", d=SLOTS, e=MEMBERS, u=2)
             nc.scalar.copy(
-                out=dst[:, :, MEMBERS * j : MEMBERS * (j + 1), :],
-                in_=y_banks[u].rearrange("p u (e d) -> p d e u", d=SLOTS),
+                out=dst[:, j + lo : j + hi, :, :, :],
+                in_=y_banks[k][:, lo:hi, :, :].rearrange("p a u (d e) -> p a d e u", d=SLOTS),
             )
 
         def quantize_y(g, c):
-            nc.vector.quantize_mx(out=y_codes[g][c][:].bitcast(FP8X4), scales=y_planes[g][:, c, :], in_=y_turned[g][c][:])
-
-        def store_codes(g, c):
+            nc.vector.quantize_mx(out=y_codes[g][c][:].bitcast(FP8X4), scales=y_planes[g][:, c, :], in_=y_turned[g, c][:])
             dst = out_1[c].rearrange("p m t -> p (m t)")[:, 4 * CHUNK * g : 4 * CHUNK * (g + 1)]
             nc.sync.dma_start(out=dst.bitcast(I32), in_=y_codes[g][c][:].bitcast(I32))
 
-        def store_scales(g, engines):
-            for q in range(4):
-                dst = out_2[:, 4 * q : 4 * q + 4, CHUNK * g : CHUNK * (g + 1)].rearrange("c r m -> r c m")
-                engines[q].dma_start(out=dst.bitcast(I32), in_=y_planes[g][32 * q : 32 * q + 4, :, :].bitcast(I32))
+        def store_scales(g, lo, hi, engines):
+            for r in range(4):
+                dst = out_2[lo:hi, r:16:4, CHUNK * g : CHUNK * (g + 1)].rearrange("c q m -> q c m")
+                engines[r].dma_start(out=dst.bitcast(I32), in_=y_planes[g][r:P:32, lo:hi, :].bitcast(I32))
 
-        def root(g, c, src):
-            roots[g, c] = work.tile([P, CHUNK], F32, name="roots", tag="roots", bufs=3)
-            nc.scalar.activation(out=roots[g, c][:], in_=src, func=ACT.Abs_reciprocal_sqrt)
+        def spread_std(g, c):
+            spreads[g, c] = psum.tile([P, CHUNK], F32, name="spread", tag="acc", bufs=4)
+            nc.tensor.matmul(
+                spreads[g, c][:], lhsT=select[g][:], rhs=std_rows[:, CHUNK * c : CHUNK * (c + 1)], start=True, stop=True
+            )
 
-        def square(g, c):
-            nc.scalar.activation(out=recip[g][c][:], in_=roots[g, c][:], func=ACT.Square)
+        def root_std(g, c):
+            recip[g, c] = keep.tile([P, CHUNK], F32, name="recip%d_%d" % (g, c))
+            nc.scalar.activation(out=recip[g, c][:], in_=spreads[g, c][:], func=ACT.Abs_reciprocal_sqrt)
 
+        def square_root(g, c):
+            nc.scalar.activation(out=recip[g, c][:], in_=recip[g, c][:], func=ACT.Square)
+
+        def clear(plane, engine):
+            engine.memset(plane[:].rearrange("p g n -> p (g n)").bitcast(I32), 0)
+
+        warm = keep.tile([P, CHUNK], BF16, name="warm")
+        nc.vector.memset(warm[:].bitcast(I32), 0)
         nc.vector.memset(one[:], 1.0)
-        nc.vector.memset(h_planes[0][:].rearrange("p g n -> p (g n)").bitcast(I32), 0)
+        clear(h_planes[0], nc.vector)
         nc.vector.memset(std_rows[:].bitcast(I32), 0)
         make_identity(nc, ident[:])
-        nc.gpsimd.memset(h_planes[1][:].rearrange("p g n -> p (g n)").bitcast(I32), 0)
         nc.scalar.activation(out=one_out[:], in_=one[:], func=ACT.Abs_reciprocal_sqrt)
+        clear(h_planes[1], nc.vector)
+        clear(h_planes[2], nc.vector)
+        for g in range(GROUPS):
+            row = STD_ROW + SLOTS * g
+            nc.vector.tensor_copy(
+                out=select[g][:].rearrange("k (e d) -> k e d", d=SLOTS),
+                in_=ident[:, row : row + SLOTS].unsqueeze(1).broadcast_to([P, MEMBERS, SLOTS]),
+            )
         nc.vector.tensor_copy(
-            out=select[:].rearrange("k (e d) -> k e d", d=SLOTS),
-            in_=ident[:, STD_ROW : STD_ROW + SLOTS].unsqueeze(1).broadcast_to([P, MEMBERS, SLOTS]),
+            out=by_slot[:].rearrange("k (d e) -> k d e", d=SLOTS), in_=ident[:].rearrange("k (e d) -> k d e", d=SLOTS)
         )
 
         load_first(0)
-        load_h(0)
-        load_h_scales(0)
-        nc.sync.dma_start(out=std_rows[STD_ROW : STD_ROW + SLOTS, :], in_=obs_std[0:SLOTS, :])
         load_first(1)
-        load_h(1)
+        nc.sync.dma_start(out=std_rows[STD_ROW : STD_ROW + T, :], in_=obs_std)
         load_a(1)
-        load_h_scales(1)
-        load_h(2)
-        load_h(3)
-        load_bias(0)
+        load_h_scales(0)
+        load_h(0)
+        load_bias(0, 0)
         load_a(2)
-        load_bias(1)
         load_a(3)
-        nc.sync.dma_start(out=std_late[:], in_=obs_std[SLOTS : 2 * SLOTS, :].unsqueeze(0).broadcast_to([MEMBERS, SLOTS, N]))
-        load_bias(2)
+        load_h_scales(1)
+        load_h(1)
+        load_bias(1, 0)
+        load_bias(0, 2)
         load_a(4)
-        load_bias(3)
-        for i in range(5, TILES):
-            load_a(i)
+        load_bias(1, 2)
+        load_h_scales(2)
+        load_h(2)
+        load_a(5)
+        load_bias(2, 0)
+        load_bias(2, 2)
+        load_a(6)
+        load_a(7)
 
+        idle = psum.tile([P, CHUNK], F32, name="idle", tag="acc", bufs=4)
+        for n in range(WARM_UPS):
+            nc.tensor.matmul(idle[:], lhsT=warm[:, :P], rhs=warm[:], start=True, stop=True)
+
+        chunks = [(g, c) for g in range(GROUPS) for c in range(CHUNKS)]
         for h in range(2):
             transpose_a(0, h)
-            evacuate_a(0, h)
-            quantize_a(0, 2 * h, 2 * h + 2)
-        for c in range(CHUNKS):
-            tag = "acc" if c == 0 else "y_bank%d" % (c - 1)
-            spread = psum.tile([P, CHUNK], F32, name="spread", tag=tag, bufs=4 if c == 0 else 1)
-            nc.tensor.matmul(spread[:], lhsT=select[:], rhs=std_rows[:, CHUNK * c : CHUNK * (c + 1)], start=True, stop=True)
-            root(0, c, spread[:])
-        for g in range(PASSES):
-            if g == 2:
-                for h in range(2):
-                    transpose_a(1, h)
-                    evacuate_a(1, h)
-                quantize_a(1, 0, PASSES)
-            for c in range(CHUNKS):
-                mx_pass(0, c, g)
-        for c in range(CHUNKS):
-            square(0, c)
-        add_bias(0)
-        add_bias(1)
-        scale(0)
-        round_y(0)
-
-        for i in range(1, TILES):
-            u = CHUNKS * i
-            last = i == TILES - 1
-            if i == 1:
-                multiply(u)
-            if not last:
-                for h in range(2):
-                    transpose_a(i + 1, h)
-                    evacuate_a(i + 1, h)
-            add_bias(u - 1)
-            scale(u - 2)
-            turned = list(range(max(u - 5, 0) if i > 2 else 0, u - 2)) if i > 1 else []
-            transpose_y(turned)
-            round_y(u - 2)
-            scale(u - 1)
-            store_y(i - 1, 0, CHUNKS)
-            round_y(u - 1)
-            for v in turned:
-                evacuate_y(v)
-            if i <= CHUNKS:
-                root(1, i - 1, std_late[:, CHUNK * (i - 1) : CHUNK * i])
-                square(1, i - 1)
-            if i >= 5:
-                quantize_y(0, i - 5)
-                store_codes(0, i - 5)
-            if i != 1:
-                multiply(u)
-            add_bias(u)
-            if not last:
-                quantize_a(i + 1, 0, PASSES)
-            else:
-                store_scales(0, [nc.sync] * 4)
-            multiply(u + 1)
-            scale(u)
-            round_y(u)
-            add_bias(u + 1)
-            multiply(u + 2)
-
-        i = TILES - 1
-        u = UNITS
-        store_y(i, 0, 1)
-        add_bias(u - 1)
-        scale(u - 2)
-        transpose_y([u - 5, u - 4, u - 3])
-        for v in range(u - 5, u - 2):
-            evacuate_y(v)
-        store_y(i, 1, 2)
-        scale(u - 1)
-        store_y(i, 2, 3)
-        round_y(u - 2)
-        round_y(u - 1)
-        quantize_y(1, 0)
-        store_codes(1, 0)
-        transpose_y([u - 2])
-        evacuate_y(u - 2)
-        quantize_y(1, 1)
-        store_codes(1, 1)
-        bank_last = psum.tile([P, 2, P], F32, name="bank_last", tag="y_bank1", bufs=1)
-        y_banks[u - 1] = bank_last[:]
+            evacuate_a(0, h, nc.vector.tensor_copy)
+        for gc in chunks[:4]:
+            spread_std(*gc)
+            root_std(*gc)
+        quantize_a(0, 0, PASSES)
         for h in range(2):
-            nc.tensor.transpose(bank_last[:, h, :], y_sorted[u - 1][:].bitcast(F32)[:, h * P : (h + 1) * P], ident[:])
-        evacuate_y(u - 1)
+            transpose_a(1, h)
+            evacuate_a(1, h, nc.vector.tensor_copy)
+        for gc in chunks[4:]:
+            spread_std(*gc)
+            root_std(*gc)
+        square_root(0, 0)
+        square_root(0, 1)
+        quantize_a(1, 0, PASSES)
+        multiply(0)
+        add_bias(0)
+        multiply(1)
+
+        a_runs = {1: [2, 3], 3: [4], 4: [5], 5: [6], 6: [7]}
+        runs = RUNS
+        square_at = {2: (0, 2), 3: (1, 0), 4: (1, 1), 5: (1, 2)}
+        turned, ready = 0, []
+        for k in range(1, PAIRS):
+            waiting, ready = ready[:1], ready[1:]
+            if k in runs:
+                for i in a_runs.get(k, []):
+                    turn_a(i)
+                for v in range(turned, min(k - LAG, turned + (0 if k == 1 else 2 if k in a_runs else 4))):
+                    transpose_y(v, 0, 2)
+                    evacuate_y(v, 0, 2)
+                    turned = v + 1
+                    if ORDER[v][2] == 2:
+                        ready.append(ORDER[v][:2])
+            add_bias(2 * k - 1)
+            scale(k - 1, 0, 1)
+            for gc in waiting:
+                quantize_y(*gc)
+            if k in runs:
+                scale(k - 1, 1, 2)
+                round_y(k - 1, 0, 2)
+            multiply(2 * k)
+            for i in a_runs.get(k, []):
+                quantize_a(i, 0, PASSES)
+            add_bias(2 * k)
+            if k not in runs:
+                scale(k - 1, 1, 2)
+                round_y(k - 1, 0, 2)
+            if k in square_at:
+                square_root(*square_at[k])
+            if k == PAIRS - 1:
+                store_scales(0, 0, CHUNKS, [nc.sync] * 4)
+            multiply(2 * k + 1)
+
+        k = PAIRS - 1
+        g, c, j = place(UNITS - 1)
+        scale(k, 0, 1)
+        round_y(k, 0, 1)
+        for v in range(turned, k):
+            transpose_y(v, 0, 2)
+            evacuate_y(v, 0, 2)
+            if ORDER[v][2] == 2:
+                ready.append(ORDER[v][:2])
+        half = CHUNK // 2
+        for h in range(2):
+            cols = slice(half * h, half * (h + 1))
+            nc.vector.tensor_tensor(out=summed[k][:, 1, cols], in0=acc[UNITS - 1][:, cols], in1=bias[j][c][:, cols], op=ALU.add)
+        for h in range(2):
+            cols = slice(half * h, half * (h + 1))
+            nc.vector.tensor_tensor(
+                out=y_sorted[k][:, CHUNK:].rearrange("t (u p e) -> t u p e", u=2, e=2)[:, :, P // 2 * h : P // 2 * (h + 1), :],
+                in0=summed[k][:, 1, cols].rearrange("t (p u e) -> t u p e", u=2, e=2),
+                in1=recip[g, c][:, cols].rearrange("t (p u e) -> t u p e", u=2, e=2),
+                op=ALU.mult,
+            )
+        transpose_y(k, 0, 2)
+        scale(k, 1, 2)
+        for gc in ready:
+            quantize_y(*gc)
+        evacuate_y(k, 0, 2)
         quantize_y(1, 2)
-        store_codes(1, 2)
-        store_scales(1, [nc.scalar, nc.scalar, nc.sync, nc.sync])
+        store_scales(1, 0, CHUNKS, [nc.scalar, nc.scalar, nc.sync, nc.sync])

@@ -30,12 +30,14 @@ PAIRS = UNITS // 2
 STD_ROW = 8
 WARM_UPS = 4
 LAG = 2
-RUNS = [1, 3, 4, 5, 6, 9, 11]
+PAIR_TO = 0
+SORT_S = {4:[0,1],5:[0],6:[0],7:[0]}
+SORT_V = {5:[1],6:[1],7:[1]}
+RUNS = [3, 4, 5, 6, 9, 11]
+ARUNS = {3: [4], 4: [5], 5: [6], 6: [7]}
 
 
-ORDER = [(0, 0, 0), (0, 1, 0), (0, 0, 2), (0, 1, 2), (0, 2, 0), (0, 2, 2)] + [
-    (1, c, j) for c in range(CHUNKS) for j in (0, 2)
-]
+ORDER = [(g, c, j) for g in range(GROUPS) for c in range(CHUNKS) for j in (0, 2)]
 
 
 def place(n):
@@ -76,7 +78,7 @@ def tile_ensemble_observation_anomalies_g4_kernel(
         ]
         y_planes = [keep.tile([P, CHUNKS, CHUNK], U8, name="y_planes%d" % g, align_bytes=64) for g in range(GROUPS)]
 
-        a_banks, grouped, spreads, recip = {}, {}, {}, {}
+        a_banks, a_sorted, grouped, spreads, recip = {}, {}, {}, {}, {}
         acc, summed, y_rows, y_sorted, y_banks, y_turned = {}, {}, {}, {}, {}, {}
 
         def load_a(i):
@@ -106,7 +108,15 @@ def tile_ensemble_observation_anomalies_g4_kernel(
             a_banks[i, h] = bank
             for g in range(2):
                 for u in range(2):
-                    nc.tensor.transpose(bank[:, g, u, :], words[:, 256 * g + u : 256 * (g + 1) : 2], ident[:])
+                    if (i, h) in a_sorted:
+                        nc.tensor.transpose(bank[:, g, u, :], a_sorted[i, h][:, g, u, :], ident[:])
+                    else:
+                        nc.tensor.transpose(bank[:, g, u, :], words[:, 256 * g + u : 256 * (g + 1) : 2], ident[:])
+
+        def sort_a(i, h, copy):
+            a_sorted[i, h] = work.tile([P, 2, 2, P], F32, name="a_sorted", tag="a_sorted", bufs=4)
+            words = raw[i][:, h * (K // 2) : (h + 1) * (K // 2)].bitcast(F32)
+            copy(out=a_sorted[i, h][:], in_=words.rearrange("t (g m u) -> t g u m", g=2, u=2))
 
         def evacuate_a(i, h, copy):
             if h == 0:
@@ -199,8 +209,8 @@ def tile_ensemble_observation_anomalies_g4_kernel(
                 dst = out_2[lo:hi, r:16:4, CHUNK * g : CHUNK * (g + 1)].rearrange("c q m -> q c m")
                 engines[r].dma_start(out=dst.bitcast(I32), in_=y_planes[g][r:P:32, lo:hi, :].bitcast(I32))
 
-        def spread_std(g, c):
-            spreads[g, c] = psum.tile([P, CHUNK], F32, name="spread", tag="acc", bufs=4)
+        def spread_std(g, c, tag):
+            spreads[g, c] = psum.tile([P, CHUNK], F32, name="spread", tag=tag, bufs=4)
             nc.tensor.matmul(
                 spreads[g, c][:], lhsT=select[g][:], rhs=std_rows[:, CHUNK * c : CHUNK * (c + 1)], start=True, stop=True
             )
@@ -218,8 +228,8 @@ def tile_ensemble_observation_anomalies_g4_kernel(
         warm = keep.tile([P, CHUNK], BF16, name="warm")
         nc.vector.memset(warm[:].bitcast(I32), 0)
         nc.vector.memset(one[:], 1.0)
-        clear(h_planes[0], nc.vector)
         nc.vector.memset(std_rows[:].bitcast(I32), 0)
+        clear(h_planes[0], nc.vector)
         make_identity(nc, ident[:])
         nc.scalar.activation(out=one_out[:], in_=one[:], func=ACT.Abs_reciprocal_sqrt)
         clear(h_planes[1], nc.vector)
@@ -240,21 +250,21 @@ def tile_ensemble_observation_anomalies_g4_kernel(
         load_a(1)
         load_h_scales(0)
         load_h(0)
-        load_bias(0, 0)
         load_a(2)
         load_a(3)
+        load_bias(0, 0)
+        load_bias(0, 2)
         load_h_scales(1)
         load_h(1)
-        load_bias(1, 0)
-        load_bias(0, 2)
         load_a(4)
+        load_bias(1, 0)
         load_bias(1, 2)
+        load_a(5)
         load_h_scales(2)
         load_h(2)
-        load_a(5)
         load_bias(2, 0)
-        load_bias(2, 2)
         load_a(6)
+        load_bias(2, 2)
         load_a(7)
 
         idle = psum.tile([P, CHUNK], F32, name="idle", tag="acc", bufs=4)
@@ -265,60 +275,71 @@ def tile_ensemble_observation_anomalies_g4_kernel(
         for h in range(2):
             transpose_a(0, h)
             evacuate_a(0, h, nc.vector.tensor_copy)
-        for gc in chunks[:4]:
-            spread_std(*gc)
+        for n, gc in enumerate(chunks[:4]):
+            spread_std(*gc, "acc" if n else "turn")
             root_std(*gc)
         quantize_a(0, 0, PASSES)
         for h in range(2):
             transpose_a(1, h)
             evacuate_a(1, h, nc.vector.tensor_copy)
         for gc in chunks[4:]:
-            spread_std(*gc)
+            spread_std(*gc, "turn")
             root_std(*gc)
         square_root(0, 0)
-        square_root(0, 1)
-        quantize_a(1, 0, PASSES)
         multiply(0)
+        quantize_a(1, 0, PASSES)
+        turn_a(2)
+        turn_a(3)
+        for gc in chunks[1:]:
+            square_root(*gc)
         add_bias(0)
+        quantize_a(2, 0, PASSES)
         multiply(1)
+        quantize_a(3, 0, PASSES)
 
-        a_runs = {1: [2, 3], 3: [4], 4: [5], 5: [6], 6: [7]}
+        a_runs = ARUNS
         runs = RUNS
-        square_at = {2: (0, 2), 3: (1, 0), 4: (1, 1), 5: (1, 2)}
         turned, ready = 0, []
         for k in range(1, PAIRS):
             waiting, ready = ready[:1], ready[1:]
             if k in runs:
                 for i in a_runs.get(k, []):
                     turn_a(i)
-                for v in range(turned, min(k - LAG, turned + (0 if k == 1 else 2 if k in a_runs else 4))):
+                for v in range(turned, min(k - (LAG if k - 1 in a_runs else 2), turned + (2 if k in a_runs else 4))):
                     transpose_y(v, 0, 2)
                     evacuate_y(v, 0, 2)
                     turned = v + 1
                     if ORDER[v][2] == 2:
                         ready.append(ORDER[v][:2])
             add_bias(2 * k - 1)
-            scale(k - 1, 0, 1)
+            for i in a_runs.get(k + 2, []):
+                for h in SORT_S.get(i, []):
+                    sort_a(i, h, nc.scalar.copy)
+            first = 0 if k <= PAIR_TO else 1
+            if first:
+                scale(k - 1, 0, 1)
             for gc in waiting:
                 quantize_y(*gc)
+            for i in a_runs.get(k + 1, []):
+                for h in SORT_V.get(i, []):
+                    sort_a(i, h, nc.vector.tensor_copy)
             if k in runs:
-                scale(k - 1, 1, 2)
+                scale(k - 1, first, 2)
                 round_y(k - 1, 0, 2)
             multiply(2 * k)
             for i in a_runs.get(k, []):
                 quantize_a(i, 0, PASSES)
             add_bias(2 * k)
             if k not in runs:
-                scale(k - 1, 1, 2)
+                scale(k - 1, first, 2)
                 round_y(k - 1, 0, 2)
-            if k in square_at:
-                square_root(*square_at[k])
             if k == PAIRS - 1:
                 store_scales(0, 0, CHUNKS, [nc.sync] * 4)
             multiply(2 * k + 1)
 
         k = PAIRS - 1
         g, c, j = place(UNITS - 1)
+        quantize_y(*ready.pop(0))
         scale(k, 0, 1)
         round_y(k, 0, 1)
         for v in range(turned, k):

@@ -29,20 +29,22 @@ UNITS = TILES * CHUNKS
 PAIRS = UNITS // 2
 STD_ROW = 8
 WARM_UPS = 4
-LAG = 2
-PAIR_TO = 0
-SORT_S = {4:[0,1],5:[0],6:[0],7:[0]}
-SORT_V = {5:[1],6:[1],7:[1]}
-RUNS = [3, 4, 5, 6, 9, 11]
-ARUNS = {3: [4], 4: [5], 5: [6], 6: [7]}
+SORT_S = {}
+A4_AT = 2
+G21 = 1
+GHELP = 1
 
 
-ORDER = [(g, c, j) for g in range(GROUPS) for c in range(CHUNKS) for j in (0, 2)]
-
-
-def place(n):
-    g, c, j = ORDER[n // 2]
-    return g, c, j + n % 2
+ORDER = [(g, c, j) for g in range(GROUPS) for c in range(CHUNKS) for j in range(TILES_PER_GROUP)]
+HELPED = [4, 7, 10, 13, 16, 19]
+A_RUNS = {5: 4, 7: 5, 9: 6, 11: 7}
+Y_RUNS = {7: [0], 9: [2], 11: [4], 14: [6, 8], 17: [10], 20: [12, 14]}
+QA_AT = {6: [4], 9: [5, 6], 12: [7]}
+QY_AT = {12: [(0, 0)], 15: [(0, 1)], 18: [(0, 2)]}
+SORT_V = {}
+SINGLE = 1
+TAIL_Y = [16, 18]
+TAIL_Q = [0, 1, 2]
 
 
 def tile_ensemble_observation_anomalies_g4_kernel(
@@ -68,6 +70,8 @@ def tile_ensemble_observation_anomalies_g4_kernel(
         h_codes = [keep.tile([P, PASSES, 2 * CHUNK], U8, name="h_codes%d" % c, align_bytes=256) for c in range(CHUNKS)]
         h_planes = [keep.tile([P, PASSES, CHUNK], U8, name="h_planes%d" % c, align_bytes=256) for c in range(CHUNKS)]
         bias = [[keep.tile([P, CHUNK], BF16, name="bias%d_%d" % (j, c)) for c in range(CHUNKS)] for j in range(TILES_PER_GROUP)]
+        recip = [keep.tile([P, N], F32, name="recip%d" % g) for g in range(GROUPS)]
+        y_turned = [keep.tile([P, CHUNKS * 4 * CHUNK], BF16, name="y_turned%d" % g, align_bytes=64) for g in range(GROUPS)]
         first_halves = [keep.tile([P, K // 2], BF16, name="first%d" % h) for h in range(2)]
         raw = [None] + [keep.tile([P, K], BF16, name="raw%d" % i) for i in range(1, TILES)]
         a_codes = [keep.tile([P, PASSES * P], U32, name="a_codes%d" % i, align_bytes=256) for i in range(TILES)]
@@ -78,8 +82,8 @@ def tile_ensemble_observation_anomalies_g4_kernel(
         ]
         y_planes = [keep.tile([P, CHUNKS, CHUNK], U8, name="y_planes%d" % g, align_bytes=64) for g in range(GROUPS)]
 
-        a_banks, a_sorted, grouped, spreads, recip = {}, {}, {}, {}, {}
-        acc, summed, y_rows, y_sorted, y_banks, y_turned = {}, {}, {}, {}, {}, {}
+        a_banks, a_sorted, grouped, spreads = {}, {}, {}, {}
+        acc, summed, y_rows, y_sorted, y_banks = {}, {}, {}, {}, {}
 
         def load_a(i):
             nc.sync.dma_start(out=raw[i][:], in_=rows_of(anomalies, *divmod(i, TILES_PER_GROUP)))
@@ -96,8 +100,8 @@ def tile_ensemble_observation_anomalies_g4_kernel(
                 src = h_scales[:, r:16:4, CHUNK * c : CHUNK * (c + 1)].rearrange("g q n -> q g n")
                 nc.sync.dma_start(out=h_planes[c][r:P:32, :, :].bitcast(I32), in_=src.bitcast(I32))
 
-        def load_bias(c, first):
-            for j in (first, first + 1):
+        def load_bias(c, tiles):
+            for j in tiles:
                 src = bias_anomalies[MEMBERS * j : MEMBERS * (j + 1), CHUNK * c : CHUNK * (c + 1)]
                 nc.sync.dma_start(out=bias[j][c][:], in_=src.unsqueeze(1).broadcast_to([MEMBERS, SLOTS, CHUNK]))
 
@@ -140,7 +144,7 @@ def tile_ensemble_observation_anomalies_g4_kernel(
             )
 
         def multiply(n):
-            g, c, j = place(n)
+            g, c, j = ORDER[n]
             i = TILES_PER_GROUP * g + j
             acc[n] = psum.tile([P, CHUNK], F32, name="acc", tag="acc", bufs=4)
             for s in range(PASSES):
@@ -155,52 +159,48 @@ def tile_ensemble_observation_anomalies_g4_kernel(
                 )
 
         def add_bias(n):
-            g, c, j = place(n)
-            if n % 2 == 0:
-                summed[n // 2] = work.tile([P, 2, CHUNK], F32, name="summed", tag="summed", bufs=3)
-            nc.vector.tensor_tensor(out=summed[n // 2][:, n % 2, :], in0=acc[n][:], in1=bias[j][c][:], op=ALU.add)
+            first, size = n - n % 2, 2
+            g, c, j = ORDER[n]
+            if n == first:
+                summed[first] = work.tile([P, size * CHUNK], F32, name="summed", tag="summed", bufs=3)
+            b = bias[j][c][:]
+            cols = slice(CHUNK * (n - first), CHUNK * (n - first + 1))
+            nc.vector.tensor_tensor(out=summed[first][:, cols], in0=acc[n][:], in1=b, op=ALU.add)
 
-        def scale(k, lo, hi):
-            g, c, j = place(2 * k)
-            if lo == 0:
-                y_rows[k] = work.tile([P, 2, CHUNK], F32, name="y_rows", tag="y_rows", bufs=6)
-            nc.vector.tensor_tensor(
-                out=y_rows[k][:, lo:hi, :],
-                in0=summed[k][:, lo:hi, :],
-                in1=recip[g, c][:].unsqueeze(1).broadcast_to([P, hi - lo, CHUNK]),
-                op=ALU.mult,
+        def scale(n, engine):
+            g, c, j = ORDER[n]
+            first = n - n % 2
+            if first not in y_rows:
+                y_rows[first] = work.tile([P, 2 * CHUNK], F32, name="y_rows", tag="y_rows", bufs=7)
+            cols = slice(CHUNK * (n % 2), CHUNK * (n % 2 + 1))
+            engine.tensor_tensor(
+                out=y_rows[first][:, cols], in0=summed[first][:, cols], in1=recip[g][:, CHUNK * c : CHUNK * (c + 1)], op=ALU.mult
             )
-            for a in range(lo, hi):
-                nc.sync.dma_start(out=rows_of(out_0, g, j + a)[:, :, CHUNK * c : CHUNK * (c + 1)], in_=y_rows[k][:, a, :])
+            nc.sync.dma_start(out=rows_of(out_0, g, j)[:, :, CHUNK * c : CHUNK * (c + 1)], in_=y_rows[first][:, cols])
 
-        def round_y(k, lo, hi):
-            if lo == 0:
-                y_sorted[k] = work.tile([P, 2 * CHUNK], BF16, name="y_sorted", tag="y_sorted", bufs=4)
+        def round_y(first, lo, hi):
+            y_sorted[first + lo] = work.tile([P, (hi - lo) * CHUNK], BF16, name="y_sorted", tag="y_sorted", bufs=6)
             nc.scalar.copy(
-                out=y_sorted[k][:, CHUNK * lo : CHUNK * hi].rearrange("t (a u p e) -> t a u p e", u=2, p=P, e=2),
-                in_=y_rows[k][:, lo:hi, :].rearrange("t a (p u e) -> t a u p e", u=2, e=2),
+                out=y_sorted[first + lo][:].rearrange("t (a u p e) -> t a u p e", u=2, p=P, e=2),
+                in_=y_rows[first][:, CHUNK * lo : CHUNK * hi].rearrange("t (a p u e) -> t a u p e", u=2, p=P, e=2),
             )
 
-        def transpose_y(k, lo, hi):
-            bank = psum.tile([P, 2, 2, P], F32, name="y_bank", tag="turn", bufs=4)
-            y_banks[k] = bank
-            words = y_sorted[k][:].bitcast(F32)
-            for a in range(lo, hi):
+        def turn_y(first, size):
+            g, c, j = ORDER[first]
+            bank = psum.tile([P, size, 2, P], F32, name="y_bank", tag="turn", bufs=4)
+            words = y_sorted[first][:].bitcast(F32)
+            for a in range(size):
                 for u in range(2):
                     nc.tensor.transpose(bank[:, a, u, :], words[:, (2 * a + u) * P : (2 * a + u + 1) * P], by_slot[:])
-
-        def evacuate_y(k, lo, hi):
-            g, c, j = place(2 * k)
-            if (g, c) not in y_turned:
-                y_turned[g, c] = work.tile([P, 4 * CHUNK], BF16, name="y_turned", tag="y_turned", bufs=3, align_bytes=64)
-            dst = y_turned[g, c][:].bitcast(F32).rearrange("p (d a e u) -> p a d e u", d=SLOTS, e=MEMBERS, u=2)
-            nc.scalar.copy(
-                out=dst[:, j + lo : j + hi, :, :, :],
-                in_=y_banks[k][:, lo:hi, :, :].rearrange("p a u (d e) -> p a d e u", d=SLOTS),
-            )
+            dst = y_turned[g][:].bitcast(F32).rearrange("p (c d j e u) -> p c j d e u", c=CHUNKS, d=SLOTS, e=MEMBERS, u=2)
+            nc.scalar.copy(out=dst[:, c, j : j + size], in_=bank[:].rearrange("p a u (d e) -> p a d e u", d=SLOTS))
 
         def quantize_y(g, c):
-            nc.vector.quantize_mx(out=y_codes[g][c][:].bitcast(FP8X4), scales=y_planes[g][:, c, :], in_=y_turned[g, c][:])
+            nc.vector.quantize_mx(
+                out=y_codes[g][c][:].bitcast(FP8X4),
+                scales=y_planes[g][:, c, :],
+                in_=y_turned[g][:, 4 * CHUNK * c : 4 * CHUNK * (c + 1)],
+            )
             dst = out_1[c].rearrange("p m t -> p (m t)")[:, 4 * CHUNK * g : 4 * CHUNK * (g + 1)]
             nc.sync.dma_start(out=dst.bitcast(I32), in_=y_codes[g][c][:].bitcast(I32))
 
@@ -216,11 +216,12 @@ def tile_ensemble_observation_anomalies_g4_kernel(
             )
 
         def root_std(g, c):
-            recip[g, c] = keep.tile([P, CHUNK], F32, name="recip%d_%d" % (g, c))
-            nc.scalar.activation(out=recip[g, c][:], in_=spreads[g, c][:], func=ACT.Abs_reciprocal_sqrt)
+            nc.scalar.activation(
+                out=recip[g][:, CHUNK * c : CHUNK * (c + 1)], in_=spreads[g, c][:], func=ACT.Abs_reciprocal_sqrt
+            )
 
-        def square_root(g, c):
-            nc.scalar.activation(out=recip[g, c][:], in_=recip[g, c][:], func=ACT.Square)
+        def square_root(g, lo, hi):
+            nc.scalar.activation(out=recip[g][:, lo:hi], in_=recip[g][:, lo:hi], func=ACT.Square)
 
         def clear(plane, engine):
             engine.memset(plane[:].rearrange("p g n -> p (g n)").bitcast(I32), 0)
@@ -252,19 +253,18 @@ def tile_ensemble_observation_anomalies_g4_kernel(
         load_h(0)
         load_a(2)
         load_a(3)
-        load_bias(0, 0)
-        load_bias(0, 2)
+        load_bias(0, range(4))
         load_h_scales(1)
         load_h(1)
         load_a(4)
-        load_bias(1, 0)
-        load_bias(1, 2)
+        load_bias(1, range(2))
+        load_bias(1, range(2, 4))
         load_a(5)
+        load_a(6)
         load_h_scales(2)
         load_h(2)
-        load_bias(2, 0)
-        load_a(6)
-        load_bias(2, 2)
+        load_bias(2, range(2))
+        load_bias(2, range(2, 4))
         load_a(7)
 
         idle = psum.tile([P, CHUNK], F32, name="idle", tag="acc", bufs=4)
@@ -285,84 +285,80 @@ def tile_ensemble_observation_anomalies_g4_kernel(
         for gc in chunks[4:]:
             spread_std(*gc, "turn")
             root_std(*gc)
-        square_root(0, 0)
+        square_root(0, 0, CHUNK)
         multiply(0)
         quantize_a(1, 0, PASSES)
         turn_a(2)
         turn_a(3)
-        for gc in chunks[1:]:
-            square_root(*gc)
+        square_root(0, CHUNK, N)
+        square_root(1, 0, N)
         add_bias(0)
         quantize_a(2, 0, PASSES)
         multiply(1)
         quantize_a(3, 0, PASSES)
-
-        a_runs = ARUNS
-        runs = RUNS
-        turned, ready = 0, []
-        for k in range(1, PAIRS):
-            waiting, ready = ready[:1], ready[1:]
-            if k in runs:
-                for i in a_runs.get(k, []):
-                    turn_a(i)
-                for v in range(turned, min(k - (LAG if k - 1 in a_runs else 2), turned + (2 if k in a_runs else 4))):
-                    transpose_y(v, 0, 2)
-                    evacuate_y(v, 0, 2)
-                    turned = v + 1
-                    if ORDER[v][2] == 2:
-                        ready.append(ORDER[v][:2])
-            add_bias(2 * k - 1)
-            for i in a_runs.get(k + 2, []):
-                for h in SORT_S.get(i, []):
-                    sort_a(i, h, nc.scalar.copy)
-            first = 0 if k <= PAIR_TO else 1
-            if first:
-                scale(k - 1, 0, 1)
-            for gc in waiting:
-                quantize_y(*gc)
-            for i in a_runs.get(k + 1, []):
-                for h in SORT_V.get(i, []):
-                    sort_a(i, h, nc.vector.tensor_copy)
-            if k in runs:
-                scale(k - 1, first, 2)
-                round_y(k - 1, 0, 2)
-            multiply(2 * k)
-            for i in a_runs.get(k, []):
+        add_bias(1)
+        scale(0, nc.vector)
+        for n in range(2, UNITS - 1):
+            if n in A_RUNS:
+                turn_a(A_RUNS[n])
+            for v in Y_RUNS.get(n, []):
+                turn_y(v, 2)
+            if n % 2 == 1:
+                round_y(n - 3, 0, 2)
+            multiply(n)
+            add_bias(n)
+            if n - 1 not in HELPED:
+                scale(n - 1, nc.vector)
+            if n in HELPED:
+                scale(n, nc.gpsimd)
+            if SINGLE and n == UNITS - 3:
+                round_y(n - 1, 0, 1)
+            for i in QA_AT.get(n, []):
                 quantize_a(i, 0, PASSES)
-            add_bias(2 * k)
-            if k not in runs:
-                scale(k - 1, first, 2)
-                round_y(k - 1, 0, 2)
-            if k == PAIRS - 1:
-                store_scales(0, 0, CHUNKS, [nc.sync] * 4)
-            multiply(2 * k + 1)
+            for gc in QY_AT.get(n, []):
+                quantize_y(*gc)
+            for i in SORT_V.get(n, []):
+                for h in range(2):
+                    sort_a(i, h, nc.vector.tensor_copy)
+            for i in SORT_S.get(n, []):
+                for h in range(2):
+                    sort_a(i, h, nc.scalar.copy)
 
-        k = PAIRS - 1
-        g, c, j = place(UNITS - 1)
-        quantize_y(*ready.pop(0))
-        scale(k, 0, 1)
-        round_y(k, 0, 1)
-        for v in range(turned, k):
-            transpose_y(v, 0, 2)
-            evacuate_y(v, 0, 2)
-            if ORDER[v][2] == 2:
-                ready.append(ORDER[v][:2])
+        n = UNITS - 1
+        g, c, j = ORDER[n]
         half = CHUNK // 2
-        for h in range(2):
-            cols = slice(half * h, half * (h + 1))
-            nc.vector.tensor_tensor(out=summed[k][:, 1, cols], in0=acc[UNITS - 1][:, cols], in1=bias[j][c][:, cols], op=ALU.add)
+        store_scales(0, 0, CHUNKS, [nc.sync] * 4)
+        multiply(n)
+        for v in TAIL_Y:
+            turn_y(v, 2)
+        if SINGLE:
+            round_y(n - 3, 1, 2)
+        else:
+            round_y(n - 3, 0, 2)
         for h in range(2):
             cols = slice(half * h, half * (h + 1))
             nc.vector.tensor_tensor(
-                out=y_sorted[k][:, CHUNK:].rearrange("t (u p e) -> t u p e", u=2, e=2)[:, :, P // 2 * h : P // 2 * (h + 1), :],
-                in0=summed[k][:, 1, cols].rearrange("t (p u e) -> t u p e", u=2, e=2),
-                in1=recip[g, c][:, cols].rearrange("t (p u e) -> t u p e", u=2, e=2),
+                out=summed[n - 1][:, CHUNK:][:, cols], in0=acc[n][:, cols], in1=bias[j][c][:, cols], op=ALU.add
+            )
+        scale(n - 1, nc.vector)
+        round_y(n - 1, 0, 1)
+        y_sorted[n] = work.tile([P, CHUNK], BF16, name="y_sorted", tag="y_sorted", bufs=6)
+        for h in range(2):
+            cols = slice(half * h, half * (h + 1))
+            nc.vector.tensor_tensor(
+                out=y_sorted[n][:].rearrange("t (u p e) -> t u p e", u=2, e=2)[:, :, P // 2 * h : P // 2 * (h + 1), :],
+                in0=summed[n - 1][:, CHUNK:][:, cols].rearrange("t (p u e) -> t u p e", u=2, e=2),
+                in1=recip[g][:, CHUNK * c :][:, cols].rearrange("t (p u e) -> t u p e", u=2, e=2),
                 op=ALU.mult,
             )
-        transpose_y(k, 0, 2)
-        scale(k, 1, 2)
-        for gc in ready:
-            quantize_y(*gc)
-        evacuate_y(k, 0, 2)
-        quantize_y(1, 2)
+        if SINGLE:
+            turn_y(n - 3, 1)
+            turn_y(n - 2, 1)
+        else:
+            turn_y(n - 3, 2)
+        turn_y(n - 1, 1)
+        turn_y(n, 1)
+        scale(n, nc.vector)
+        for c in TAIL_Q:
+            quantize_y(1, c)
         store_scales(1, 0, CHUNKS, [nc.scalar, nc.scalar, nc.sync, nc.sync])

from contextlib import ExitStack

import concourse.mybir as mybir
from concourse.masks import make_identity

T, R, K, N = 8, 128, 2048, 1536
FLOPS = 2 * T * R * K * N

F32 = mybir.dt.float32
BF16 = mybir.dt.bfloat16
I32 = mybir.dt.int32
U32 = mybir.dt.uint32
U8 = mybir.dt.uint8
FP8X4 = mybir.dt.float8_e4m3fn_x4
FP4X4 = mybir.dt.float4_e2m1fn_x4
ACT = mybir.ActivationFunctionType
ALU = mybir.AluOpType

P = 128
PASSES = K // 512
CHUNK = 512
CHUNKS = N // CHUNK
SLOTS = 4
MEMBERS = P // SLOTS
GROUPS = T // SLOTS
TILES_PER_GROUP = R // MEMBERS
TILES = GROUPS * TILES_PER_GROUP
UNITS = TILES * CHUNKS
PAIRS = UNITS // 2
STD_ROW = 8
WARM_UPS = 4
SORT_S = {}
A4_AT = 2
G21 = 1
GHELP = 1


ORDER = [(g, c, j) for g in range(GROUPS) for c in range(CHUNKS) for j in range(TILES_PER_GROUP)]
HELPED = [4, 7, 10, 13, 16, 19]
A_RUNS = {5: 4, 7: 5, 9: 6, 11: 7}
Y_RUNS = {7: [0], 9: [2], 11: [4], 14: [6, 8], 17: [10], 20: [12, 14]}
QA_AT = {6: [4], 9: [5, 6], 12: [7]}
QY_AT = {12: [(0, 0)], 15: [(0, 1)], 18: [(0, 2)]}
SORT_V = {}
SINGLE = 1
TAIL_Y = [16, 18]
TAIL_Q = [0, 1, 2]


def tile_ensemble_observation_anomalies_g4_kernel(
    tc, anomalies, h_words, h_scales, bias_anomalies, obs_std, out_0, out_1, out_2
):
    nc = tc.nc

    def rows_of(tensor, g, j):
        return tensor[SLOTS * g : SLOTS * (g + 1), MEMBERS * j : MEMBERS * (j + 1), :].rearrange("d e x -> e d x")

    with ExitStack() as ctx:
        keep = ctx.enter_context(tc.tile_pool(name="keep", bufs=1))
        work = ctx.enter_context(tc.tile_pool(name="work", bufs=1))
        psum = ctx.enter_context(tc.psum_pool(name="psum", bufs=1))
        ctx.enter_context(tc.manual_schedule())

        ident = keep.tile([P, P], F32, name="ident")
        by_slot = keep.tile([P, P], F32, name="by_slot")
        select = [keep.tile([P, P], BF16, name="select%d" % g) for g in range(GROUPS)]
        one = keep.tile([P, 1], F32, name="one")
        one_out = keep.tile([P, 1], F32, name="one_out")
        std_rows = keep.tile([P, N], BF16, name="std_rows")
        h_codes = [keep.tile([P, PASSES, 2 * CHUNK], U8, name="h_codes%d" % c, align_bytes=256) for c in range(CHUNKS)]
        h_planes = [keep.tile([P, PASSES, CHUNK], U8, name="h_planes%d" % c, align_bytes=256) for c in range(CHUNKS)]
        bias = [[keep.tile([P, CHUNK], BF16, name="bias%d_%d" % (j, c)) for c in range(CHUNKS)] for j in range(TILES_PER_GROUP)]
        recip = [keep.tile([P, N], F32, name="recip%d" % g) for g in range(GROUPS)]
        y_turned = [keep.tile([P, CHUNKS * 4 * CHUNK], BF16, name="y_turned%d" % g, align_bytes=64) for g in range(GROUPS)]
        first_halves = [keep.tile([P, K // 2], BF16, name="first%d" % h) for h in range(2)]
        raw = [None] + [keep.tile([P, K], BF16, name="raw%d" % i) for i in range(1, TILES)]
        a_codes = [keep.tile([P, PASSES * P], U32, name="a_codes%d" % i, align_bytes=256) for i in range(TILES)]
        a_planes = [keep.tile([P, PASSES * P], U8, name="a_planes%d" % i, align_bytes=256) for i in range(TILES)]
        y_codes = [
            [keep.tile([P, CHUNK], U32, name="y_codes%d_%d" % (g, c), align_bytes=64) for c in range(CHUNKS)]
            for g in range(GROUPS)
        ]
        y_planes = [keep.tile([P, CHUNKS, CHUNK], U8, name="y_planes%d" % g, align_bytes=64) for g in range(GROUPS)]

        a_banks, a_sorted, grouped, spreads = {}, {}, {}, {}
        acc, summed, y_rows, y_sorted, y_banks = {}, {}, {}, {}, {}

        def load_a(i):
            nc.sync.dma_start(out=raw[i][:], in_=rows_of(anomalies, *divmod(i, TILES_PER_GROUP)))

        def load_first(h):
            nc.sync.dma_start(out=first_halves[h][:], in_=rows_of(anomalies, 0, 0)[:, :, h * (K // 2) : (h + 1) * (K // 2)])

        def load_h(c):
            src = h_words[:, :, 2 * CHUNK * c : 2 * CHUNK * (c + 1)].rearrange("g p x -> p g x")
            nc.sync.dma_start(out=h_codes[c][:].bitcast(I32), in_=src.bitcast(I32))

        def load_h_scales(c):
            for r in range(4):
                src = h_scales[:, r:16:4, CHUNK * c : CHUNK * (c + 1)].rearrange("g q n -> q g n")
                nc.sync.dma_start(out=h_planes[c][r:P:32, :, :].bitcast(I32), in_=src.bitcast(I32))

        def load_bias(c, tiles):
            for j in tiles:
                src = bias_anomalies[MEMBERS * j : MEMBERS * (j + 1), CHUNK * c : CHUNK * (c + 1)]
                nc.sync.dma_start(out=bias[j][c][:], in_=src.unsqueeze(1).broadcast_to([MEMBERS, SLOTS, CHUNK]))

        def transpose_a(i, h):
            src = first_halves[h][:] if i == 0 else raw[i][:, h * (K // 2) : (h + 1) * (K // 2)]
            words = src.bitcast(F32)
            bank = psum.tile([P, 2, 2, P], F32, name="a_bank", tag="turn", bufs=4)
            a_banks[i, h] = bank
            for g in range(2):
                for u in range(2):
                    if (i, h) in a_sorted:
                        nc.tensor.transpose(bank[:, g, u, :], a_sorted[i, h][:, g, u, :], ident[:])
                    else:
                        nc.tensor.transpose(bank[:, g, u, :], words[:, 256 * g + u : 256 * (g + 1) : 2], ident[:])

        def sort_a(i, h, copy):
            a_sorted[i, h] = work.tile([P, 2, 2, P], F32, name="a_sorted", tag="a_sorted", bufs=4)
            words = raw[i][:, h * (K // 2) : (h + 1) * (K // 2)].bitcast(F32)
            copy(out=a_sorted[i, h][:], in_=words.rearrange("t (g m u) -> t g u m", g=2, u=2))

        def evacuate_a(i, h, copy):
            if h == 0:
                grouped[i] = work.tile([P, K], BF16, name="grouped", tag="grouped", bufs=3, align_bytes=64)
            dst = grouped[i][:, h * (K // 2) : (h + 1) * (K // 2)].bitcast(F32)
            copy(
                out=dst.rearrange("p (g r u) -> p g r u", g=2, u=2),
                in_=a_banks[i, h][:].rearrange("p g u r -> p g r u"),
            )

        def turn_a(i):
            for h in range(2):
                transpose_a(i, h)
                evacuate_a(i, h, nc.scalar.copy)

        def quantize_a(i, lo, hi):
            nc.vector.quantize_mx(
                out=a_codes[i][:, lo * P : hi * P].bitcast(FP8X4),
                scales=a_planes[i][:, lo * P : hi * P],
                in_=grouped[i][:, lo * 4 * P : hi * 4 * P],
            )

        def multiply(n):
            g, c, j = ORDER[n]
            i = TILES_PER_GROUP * g + j
            acc[n] = psum.tile([P, CHUNK], F32, name="acc", tag="acc", bufs=4)
            for s in range(PASSES):
                nc.tensor.matmul_mx(
                    out=acc[n][:],
                    lhsT=a_codes[i][:, s * P : (s + 1) * P].bitcast(FP8X4),
                    lhsT_scale=a_planes[i][:, s * P : (s + 1) * P],
                    rhs=h_codes[c][:, s, :].bitcast(FP4X4),
                    rhs_scale=h_planes[c][:, s, :],
                    start=(s == 0),
                    stop=(s == PASSES - 1),
                )

        def add_bias(n):
            first, size = n - n % 2, 2
            g, c, j = ORDER[n]
            if n == first:
                summed[first] = work.tile([P, size * CHUNK], F32, name="summed", tag="summed", bufs=3)
            b = bias[j][c][:]
            cols = slice(CHUNK * (n - first), CHUNK * (n - first + 1))
            nc.vector.tensor_tensor(out=summed[first][:, cols], in0=acc[n][:], in1=b, op=ALU.add)

        def scale(n, engine):
            g, c, j = ORDER[n]
            first = n - n % 2
            if first not in y_rows:
                y_rows[first] = work.tile([P, 2 * CHUNK], F32, name="y_rows", tag="y_rows", bufs=7)
            cols = slice(CHUNK * (n % 2), CHUNK * (n % 2 + 1))
            engine.tensor_tensor(
                out=y_rows[first][:, cols], in0=summed[first][:, cols], in1=recip[g][:, CHUNK * c : CHUNK * (c + 1)], op=ALU.mult
            )
            nc.sync.dma_start(out=rows_of(out_0, g, j)[:, :, CHUNK * c : CHUNK * (c + 1)], in_=y_rows[first][:, cols])

        def round_y(first, lo, hi):
            y_sorted[first + lo] = work.tile([P, (hi - lo) * CHUNK], BF16, name="y_sorted", tag="y_sorted", bufs=6)
            nc.scalar.copy(
                out=y_sorted[first + lo][:].rearrange("t (a u p e) -> t a u p e", u=2, p=P, e=2),
                in_=y_rows[first][:, CHUNK * lo : CHUNK * hi].rearrange("t (a p u e) -> t a u p e", u=2, p=P, e=2),
            )

        def turn_y(first, size):
            g, c, j = ORDER[first]
            bank = psum.tile([P, size, 2, P], F32, name="y_bank", tag="turn", bufs=4)
            words = y_sorted[first][:].bitcast(F32)
            for a in range(size):
                for u in range(2):
                    nc.tensor.transpose(bank[:, a, u, :], words[:, (2 * a + u) * P : (2 * a + u + 1) * P], by_slot[:])
            dst = y_turned[g][:].bitcast(F32).rearrange("p (c d j e u) -> p c j d e u", c=CHUNKS, d=SLOTS, e=MEMBERS, u=2)
            nc.scalar.copy(out=dst[:, c, j : j + size], in_=bank[:].rearrange("p a u (d e) -> p a d e u", d=SLOTS))

        def quantize_y(g, c):
            nc.vector.quantize_mx(
                out=y_codes[g][c][:].bitcast(FP8X4),
                scales=y_planes[g][:, c, :],
                in_=y_turned[g][:, 4 * CHUNK * c : 4 * CHUNK * (c + 1)],
            )
            dst = out_1[c].rearrange("p m t -> p (m t)")[:, 4 * CHUNK * g : 4 * CHUNK * (g + 1)]
            nc.sync.dma_start(out=dst.bitcast(I32), in_=y_codes[g][c][:].bitcast(I32))

        def store_scales(g, lo, hi, engines):
            for r in range(4):
                dst = out_2[lo:hi, r:16:4, CHUNK * g : CHUNK * (g + 1)].rearrange("c q m -> q c m")
                engines[r].dma_start(out=dst.bitcast(I32), in_=y_planes[g][r:P:32, lo:hi, :].bitcast(I32))

        def spread_std(g, c, tag):
            spreads[g, c] = psum.tile([P, CHUNK], F32, name="spread", tag=tag, bufs=4)
            nc.tensor.matmul(
                spreads[g, c][:], lhsT=select[g][:], rhs=std_rows[:, CHUNK * c : CHUNK * (c + 1)], start=True, stop=True
            )

        def root_std(g, c):
            nc.scalar.activation(
                out=recip[g][:, CHUNK * c : CHUNK * (c + 1)], in_=spreads[g, c][:], func=ACT.Abs_reciprocal_sqrt
            )

        def square_root(g, lo, hi):
            nc.scalar.activation(out=recip[g][:, lo:hi], in_=recip[g][:, lo:hi], func=ACT.Square)

        def clear(plane, engine):
            engine.memset(plane[:].rearrange("p g n -> p (g n)").bitcast(I32), 0)

        warm = keep.tile([P, CHUNK], BF16, name="warm")
        nc.vector.memset(warm[:].bitcast(I32), 0)
        nc.vector.memset(one[:], 1.0)
        nc.vector.memset(std_rows[:].bitcast(I32), 0)
        clear(h_planes[0], nc.vector)
        make_identity(nc, ident[:])
        nc.scalar.activation(out=one_out[:], in_=one[:], func=ACT.Abs_reciprocal_sqrt)
        clear(h_planes[1], nc.vector)
        clear(h_planes[2], nc.vector)
        for g in range(GROUPS):
            row = STD_ROW + SLOTS * g
            nc.vector.tensor_copy(
                out=select[g][:].rearrange("k (e d) -> k e d", d=SLOTS),
                in_=ident[:, row : row + SLOTS].unsqueeze(1).broadcast_to([P, MEMBERS, SLOTS]),
            )
        nc.vector.tensor_copy(
            out=by_slot[:].rearrange("k (d e) -> k d e", d=SLOTS), in_=ident[:].rearrange("k (e d) -> k d e", d=SLOTS)
        )

        load_first(0)
        load_first(1)
        nc.sync.dma_start(out=std_rows[STD_ROW : STD_ROW + T, :], in_=obs_std)
        load_a(1)
        load_h_scales(0)
        load_h(0)
        load_a(2)
        load_a(3)
        load_bias(0, range(4))
        load_h_scales(1)
        load_h(1)
        load_a(4)
        load_bias(1, range(2))
        load_bias(1, range(2, 4))
        load_a(5)
        load_a(6)
        load_h_scales(2)
        load_h(2)
        load_bias(2, range(2))
        load_bias(2, range(2, 4))
        load_a(7)

        idle = psum.tile([P, CHUNK], F32, name="idle", tag="acc", bufs=4)
        for n in range(WARM_UPS):
            nc.tensor.matmul(idle[:], lhsT=warm[:, :P], rhs=warm[:], start=True, stop=True)

        chunks = [(g, c) for g in range(GROUPS) for c in range(CHUNKS)]
        for h in range(2):
            transpose_a(0, h)
            evacuate_a(0, h, nc.vector.tensor_copy)
        for n, gc in enumerate(chunks[:4]):
            spread_std(*gc, "acc" if n else "turn")
            root_std(*gc)
        quantize_a(0, 0, PASSES)
        for h in range(2):
            transpose_a(1, h)
            evacuate_a(1, h, nc.vector.tensor_copy)
        for gc in chunks[4:]:
            spread_std(*gc, "turn")
            root_std(*gc)
        square_root(0, 0, CHUNK)
        multiply(0)
        quantize_a(1, 0, PASSES)
        turn_a(2)
        turn_a(3)
        square_root(0, CHUNK, N)
        square_root(1, 0, N)
        add_bias(0)
        quantize_a(2, 0, PASSES)
        multiply(1)
        quantize_a(3, 0, PASSES)
        add_bias(1)
        scale(0, nc.vector)
        for n in range(2, UNITS - 1):
            if n in A_RUNS:
                turn_a(A_RUNS[n])
            for v in Y_RUNS.get(n, []):
                turn_y(v, 2)
            if n % 2 == 1:
                round_y(n - 3, 0, 2)
            multiply(n)
            add_bias(n)
            if n - 1 not in HELPED:
                scale(n - 1, nc.vector)
            if n in HELPED:
                scale(n, nc.gpsimd)
            if SINGLE and n == UNITS - 3:
                round_y(n - 1, 0, 1)
            for i in QA_AT.get(n, []):
                quantize_a(i, 0, PASSES)
            for gc in QY_AT.get(n, []):
                quantize_y(*gc)
            for i in SORT_V.get(n, []):
                for h in range(2):
                    sort_a(i, h, nc.vector.tensor_copy)
            for i in SORT_S.get(n, []):
                for h in range(2):
                    sort_a(i, h, nc.scalar.copy)

        n = UNITS - 1
        g, c, j = ORDER[n]
        half = CHUNK // 2
        store_scales(0, 0, CHUNKS, [nc.sync] * 4)
        multiply(n)
        for v in TAIL_Y:
            turn_y(v, 2)
        if SINGLE:
            round_y(n - 3, 1, 2)
        else:
            round_y(n - 3, 0, 2)
        for h in range(2):
            cols = slice(half * h, half * (h + 1))
            nc.vector.tensor_tensor(
                out=summed[n - 1][:, CHUNK:][:, cols], in0=acc[n][:, cols], in1=bias[j][c][:, cols], op=ALU.add
            )
        scale(n - 1, nc.vector)
        round_y(n - 1, 0, 1)
        y_sorted[n] = work.tile([P, CHUNK], BF16, name="y_sorted", tag="y_sorted", bufs=6)
        for h in range(2):
            cols = slice(half * h, half * (h + 1))
            nc.vector.tensor_tensor(
                out=y_sorted[n][:].rearrange("t (u p e) -> t u p e", u=2, e=2)[:, :, P // 2 * h : P // 2 * (h + 1), :],
                in0=summed[n - 1][:, CHUNK:][:, cols].rearrange("t (p u e) -> t u p e", u=2, e=2),
                in1=recip[g][:, CHUNK * c :][:, cols].rearrange("t (p u e) -> t u p e", u=2, e=2),
                op=ALU.mult,
            )
        if SINGLE:
            turn_y(n - 3, 1)
            turn_y(n - 2, 1)
        else:
            turn_y(n - 3, 2)
        turn_y(n - 1, 1)
        turn_y(n, 1)
        scale(n, nc.vector)
        for c in TAIL_Q:
            quantize_y(1, c)
        store_scales(1, 0, CHUNKS, [nc.scalar, nc.scalar, nc.sync, nc.sync])
